import numpy as np
import ml_dtypes


def mxq(x, axis, fmt="e4m3"):
    dtype, down = {"e4m3": (ml_dtypes.float8_e4m3fn, 7), "e5m2": (ml_dtypes.float8_e5m2, 14)}[fmt]
    v = np.moveaxis(np.asarray(x, np.float32).astype(ml_dtypes.bfloat16).astype(np.float64), axis, -1)
    blocks = v.reshape(v.shape[:-1] + (-1, 32))
    amax = np.abs(blocks).max(-1, keepdims=True)
    byte = np.maximum(np.where(amax > 0, np.frexp(amax)[1] - 1 + 127, 0) - down, 1)
    scale = np.exp2(byte - 127.0)
    codes = (blocks / scale).astype(np.float32).astype(dtype).astype(np.float64)
    return np.moveaxis((codes * scale).reshape(v.shape), -1, axis)


WIDE = False


def mx_kscale(k):
    if not WIDE:
        return np.ones(k)
    levels = np.array([10, -10, 5, -5, 0])
    if k % 512:
        return np.exp2(np.random.permutation(np.resize(levels, k // 32))).repeat(32)
    a = np.empty((k // 512, 16))
    for p in range(k // 512):
        a[p, :8] = np.random.permutation(np.resize(levels, 8))
        for g in range(8):
            far = levels[np.abs(levels - a[p, g]) >= 10]
            a[p, g + 8] = far[np.random.randint(len(far))]
    return np.exp2(a.ravel()).repeat(32)


def f64(x):
    return np.asarray(x).astype(np.float64)


def striped(idx):
    return np.tile(idx.reshape(-1, 16).T, (8, 1)).astype(np.uint16)


def unstriped(offs):
    return offs[:16].T.reshape(-1).astype(np.int64)


def pack_weight(w):
    k, n = w.shape
    w = f64(np.asarray(w, np.float32).astype(ml_dtypes.bfloat16)).reshape(k // 32, 32, n)
    amax = np.abs(w).max(1)
    byte = np.clip(np.where(amax > 0, np.frexp(amax)[1] - 1 + 127 - 7, 1), 1, 254)
    scaled = (w * np.exp2(127.0 - byte)[:, None, :]).reshape(k, n).astype(np.float32)
    words = np.ascontiguousarray(scaled.reshape(k // 512, 128, 4, n).transpose(0, 1, 3, 2)).astype(ml_dtypes.float8_e4m3fn).view(np.uint8)
    return words, np.ascontiguousarray(byte.astype(np.uint8).reshape(k // 512, 16, n))


def unpack_weight(words, scales):
    g, p, n, _ = words.shape
    vals = np.ascontiguousarray(words).view(ml_dtypes.float8_e4m3fn).astype(np.float64) * np.repeat(np.exp2(scales.astype(np.float64) - 127.0), 8, axis=1)[..., None]
    return vals.transpose(0, 1, 3, 2).reshape(g * 512, n)


def gelu(v):
    return 0.5 * v * (1.0 + np.tanh(np.sqrt(2.0 / np.pi) * (v + 0.044715 * v**3)))


K, T, S, V, H = 1024, 2048, 512, 512, 512
P = 2 ** 7


def setup_inputs():
    n = np.random.standard_normal
    s = mx_kscale(K)[:, None]
    u = mx_kscale(H)
    packed_xT = pack_weight(n((K, T)) * s)
    return {
        "x_words": packed_xT[0],
        "x_scales": packed_xT[1],
        "w1": (n((K, H)) / np.sqrt(K) / s * u).astype(np.float32),
        "w2": (n((K, H)) / np.sqrt(K) / s / u / np.sqrt(H)).astype(np.float32),
        "head": (np.tile(0.5 * np.random.standard_normal(T), (P, 1))).astype(np.float32),
        "offs": striped(np.random.permutation(T)[:S]),
        "dst": striped(np.random.permutation(T)[:V]),
    }


def reference(x_words, x_scales, w1, w2, head, offs, dst):
    xq = unpack_weight(x_words, x_scales)[:, unstriped(offs)]
    p = gelu(mxq(f64(w1), 0, "e4m3").T @ xq)
    x_dst = unpack_weight(x_words, x_scales)[:, unstriped(dst)]
    d = gelu(mxq(f64(w2), 0, "e4m3").T @ x_dst)
    y = (mxq(p, 0, "e4m3").T @ mxq(d, 0, "e4m3")) + f64(head)[:1][:, unstriped(dst)]
    e = np.exp(y - y.max(axis=1, keepdims=True))
    return e / e.sum(axis=1, keepdims=True)

@@ -1,0 +1,233 @@
+from contextlib import ExitStack
+
+import concourse.mybir as mybir
+
+K, T, S, H = 1024, 2048, 512, 512
+FLOPS = 2 * (2 * K * H * S) + 2 * H * S * S
+
+F32 = mybir.dt.float32
+BF16 = mybir.dt.bfloat16
+I32 = mybir.dt.int32
+U32 = mybir.dt.uint32
+U16 = mybir.dt.uint16
+U8 = mybir.dt.uint8
+FP8X4 = mybir.dt.float8_e4m3fn_x4
+ACT = mybir.ActivationFunctionType
+ALU = mybir.AluOpType
+AXIS = mybir.AxisListType
+
+P = 128
+PACK = 4
+K_PASS = P * PACK
+PASSES = K // K_PASS
+CHUNK = 128
+CHUNKS = S // CHUNK
+HALF = S // 2
+SLOT = 4 * T
+
+
+def tile_picked_zarc_gelu_p_kernel(tc, x_words, x_scales, w1, w2, head, offs, dst, out):
+    nc = tc.nc
+    with ExitStack() as ctx:
+        keep = ctx.enter_context(tc.tile_pool(name="keep", bufs=1))
+        stage = ctx.enter_context(tc.tile_pool(name="stage", bufs=1))
+        psum = ctx.enter_context(tc.psum_pool(name="psum", bufs=1))
+
+        def sb(name, shape, dtype, tag=None):
+            return keep.tile(shape, dtype, name=name, tag=tag or name, align_bytes=64)
+
+        def bank(name, tag):
+            return psum.tile([P, S], F32, name=name, tag=tag)
+
+        offs_sb = keep.tile([P, S // 16], U16, name="offs_sb")
+        dst_sb = keep.tile([P, S // 16], U16, name="dst_sb")
+        nc.sync.dma_start(offs_sb[:], offs)
+        nc.sync.dma_start(dst_sb[:], dst)
+
+        scale_table = sb("scale_table", [P, T], U8)
+        nc.vector.memset(scale_table[:].bitcast(I32), 0)
+        for q in range(4):
+            nc.scalar.dma_start(
+                out=scale_table[32 * q : 32 * q + 4 * PASSES, :].bitcast(I32),
+                in_=x_scales[:, 4 * q : 4 * q + 4, :].bitcast(I32),
+            )
+        head_table = sb("head_table", [P, T], F32)
+        nc.vector.memset(head_table[:], 0.0)
+        nc.sync.dma_start(out=head_table[0:1, :], in_=head[0:1, :])
+        ident = sb("ident", [P, P], F32)
+        zeros = stage.tile([P, 3 * T], F32, name="zeros", offset=SLOT)
+        nc.vector.memset(zeros[:, 0:P], 0.0)
+        nc.gpsimd.affine_select(
+            out=ident[:],
+            in_=zeros[:, 0:P],
+            compare_op=ALU.not_equal,
+            fill=1.0,
+            base=0,
+            pattern=[[-1, P]],
+            channel_multiplier=1,
+        )
+
+        def load_words(o, offset):
+            table = stage.tile([P, T], U32, name=f"word_table{o}", offset=offset)
+            nc.sync.dma_start(
+                out=table[:].bitcast(I32),
+                in_=x_words[o].rearrange("p n r -> p (n r)").bitcast(I32),
+            )
+            return table
+
+        def load_weight(name, offset, w, o, c0, c1):
+            raw = stage.tile([P, PACK, c1 - c0], F32, name=name, offset=offset)
+            rows = w[o * K_PASS : (o + 1) * K_PASS, c0:c1]
+            nc.sync.dma_start(out=raw[:], in_=rows.rearrange("(p j) c -> p j c", j=PACK))
+            return raw
+
+        def load_halves(name, offset, w):
+            return [load_weight(f"{name}{h}", offset + h * SLOT // 2, w, 1, h * H // 2, (h + 1) * H // 2) for h in range(2)]
+
+        def round_weight(name, raw, vector_units):
+            width = raw.shape[2]
+            units = width // 16
+            rounded = sb(name, [P, PACK * width], BF16)
+            src = raw[:].rearrange("p j (u t i) -> p u t j i", t=4, i=4)
+            dst_view = rounded[:].rearrange("p (t u i j) -> p u t j i", t=4, i=4, j=4)
+            if vector_units > 0:
+                nc.vector.tensor_copy(out=dst_view[:, 0:vector_units], in_=src[:, 0:vector_units])
+            if vector_units < units:
+                nc.scalar.copy(out=dst_view[:, vector_units:units], in_=src[:, vector_units:units])
+            return rounded
+
+        def mx_tiles(name, width):
+            return sb(name + "_codes", [P, width], U32), sb(name + "_scales", [P, width], U8)
+
+        def quantize(mx, c0, c1, values):
+            nc.vector.quantize_mx(out=mx[0][:, c0:c1].bitcast(FP8X4), scales=mx[1][:, c0:c1], in_=values)
+
+        def quantize_half(mx, h, rounded):
+            for t in range(PACK):
+                c0 = t * P + h * P // 2
+                quantize(mx, c0, c0 + P // 2, rounded[:, t * 256 : (t + 1) * 256])
+
+        def gather(name, table, dtype, lst):
+            picked = sb(name, [P, 16 * lst.shape[1]], dtype)
+            nc.vector.tensor_copy(out=picked[:], in_=table[:].indirect(lst))
+            return picked
+
+        def gather_half(name, table, lst, h):
+            return gather(f"{name}{h}", table, U32, lst[:, 16 * h : 16 * (h + 1)])
+
+        w2_mx = [mx_tiles(f"w2_mx{o}", H) for o in range(PASSES)]
+        w1_mx = [mx_tiles(f"w1_mx{o}", H) for o in range(PASSES)]
+
+        w1_raw0 = load_weight("w1_raw0", 0, w1, 0, 0, H)
+        words0 = load_words(0, SLOT)
+        w2_raw0 = load_weight("w2_raw0", 2 * SLOT, w2, 0, 0, H)
+        words1 = load_words(1, 3 * SLOT)
+
+        w1_bf0 = round_weight("w1_bf0", w1_raw0, 0)
+        w2_raw1 = load_halves("w2_raw1", 0, w2)
+        d_scales = gather("d_scales", scale_table, U8, dst_sb[:])
+        p_scales = gather("p_scales", scale_table, U8, offs_sb[:])
+        head_row = gather("head_row", head_table, F32, dst_sb[:])
+
+        turned = bank("turned", "p0")
+        for c in range(CHUNKS):
+            nc.tensor.transpose(turned[:, c * P : (c + 1) * P], head_row[:, c * P : (c + 1) * P], ident[:])
+        head_col = sb("head_col", [P, CHUNKS], F32)
+        nc.scalar.copy(out=head_col[:], in_=turned[:, 0:S:P])
+        spread = bank("spread", "p1")
+        for c in range(CHUNKS):
+            nc.tensor.transpose(spread[:, c * P : (c + 1) * P], head_col[:, c : c + 1].to_broadcast([P, P]), ident[:])
+        head_all = sb("head_all", [P, S], F32)
+        nc.scalar.copy(out=head_all[:], in_=spread[:])
+
+        d_words0 = gather("d_words0", words0, U32, dst_sb[:])
+        p_words0 = gather("p_words0", words0, U32, offs_sb[:])
+        quantize(w1_mx[0], 0, H, w1_bf0[:])
+        w2_bf0 = round_weight("w2_bf0", w2_raw0, 6)
+        w1_raw1 = load_halves("w1_raw1", 2 * SLOT, w1)
+        quantize(w2_mx[0], 0, H, w2_bf0[:])
+        d_words1 = [gather_half("d_words1", words1, dst_sb, h) for h in range(2)]
+        p_words1 = [gather_half("p_words1", words1, offs_sb, 0)]
+        for i in range(8):
+            warm = bank(f"warm{i}", f"p{2 + i % 2}")
+            nc.tensor.matmul_mx(
+                out=warm[:, 0:HALF],
+                lhsT=w2_mx[0][0][:, 0:P].bitcast(FP8X4),
+                lhsT_scale=w2_mx[0][1][:, 0:P],
+                rhs=d_words1[1][:].bitcast(FP8X4),
+                rhs_scale=d_scales[4:P, 1 * HALF : (1 + 1) * HALF],
+                start=True,
+                stop=True,
+            )
+        for h, vector_units in enumerate((0, 8)):
+            quantize_half(w2_mx[1], h, round_weight(f"w2_bf1{h}", w2_raw1[h], vector_units))
+
+        def tower_chunk(acc, w_mx, picked0, picked1, picked_scales, c, hidden):
+            cols = slice(c * CHUNK, (c + 1) * CHUNK)
+            moving = (picked0[:, cols], picked1[c // 2][:, (c % 2) * CHUNK : (c % 2 + 1) * CHUNK])
+            for t in range(PACK):
+                for o in range(PASSES):
+                    nc.tensor.matmul_mx(
+                        out=acc[:, t * CHUNK : (t + 1) * CHUNK],
+                        lhsT=w_mx[o][0][:, t * P : (t + 1) * P].bitcast(FP8X4),
+                        lhsT_scale=w_mx[o][1][:, t * P : (t + 1) * P],
+                        rhs=moving[o].bitcast(FP8X4),
+                        rhs_scale=picked_scales[4 * o : P, cols],
+                        start=(o == 0),
+                        stop=(o == PASSES - 1),
+                    )
+            nc.scalar.activation(
+                out=hidden.rearrange("p (n t) -> p n t", t=PACK),
+                in_=acc[:].rearrange("p (t n) -> p n t", t=PACK),
+                func=ACT.Gelu_apprx_tanh,
+            )
+
+        d_bf = [sb(f"d_bf{h}", [P, PACK * HALF], BF16) for h in range(2)]
+        for c in range(CHUNKS):
+            part = d_bf[c // 2][:, (c % 2) * K_PASS : (c % 2 + 1) * K_PASS]
+            tower_chunk(bank(f"d_acc{c}", f"d{c}"), w2_mx, d_words0, d_words1, d_scales, c, part)
+
+        for h, vector_units in enumerate((16, 16)):
+            quantize_half(w1_mx[1], h, round_weight(f"w1_bf1{h}", w1_raw1[h], vector_units))
+        p_words1.append(gather_half("p_words1", words1, offs_sb, 1))
+
+        d_mx = mx_tiles("d_mx", S)
+        for h in range(2):
+            quantize(d_mx, h * HALF, (h + 1) * HALF, d_bf[h][:])
+
+        p_bf = [sb(f"p_bf{c}", [P, K_PASS], BF16, tag="late" if c == CHUNKS - 1 else None) for c in range(CHUNKS)]
+        p_mx = [mx_tiles(f"p_mx{c}", CHUNK) for c in range(CHUNKS)]
+        logits = [sb(f"logits{c}", [P, S], F32) for c in range(CHUNKS)]
+        neg_max = [sb(f"neg_max{c}", [P, 1], F32) for c in range(CHUNKS)]
+
+        def scores(c):
+            quantize(p_mx[c], 0, CHUNK, p_bf[c][:])
+            acc = bank(f"y_acc{c}", f"d{c}")
+            nc.tensor.matmul_mx(
+                out=acc[:],
+                lhsT=p_mx[c][0][:].bitcast(FP8X4),
+                lhsT_scale=p_mx[c][1][:],
+                rhs=d_mx[0][:].bitcast(FP8X4),
+                rhs_scale=d_mx[1][:],
+                start=True,
+                stop=True,
+            )
+            nc.vector.tensor_tensor(out=logits[c][:], in0=acc[:], in1=head_all[:], op=ALU.add)
+            nc.vector.tensor_reduce(out=neg_max[c][:], in_=logits[c][:], axis=AXIS.X, op=ALU.max, negate=True)
+
+        for c in range(CHUNKS):
+            tower_chunk(bank(f"p_acc{c}", f"p{c}"), w1_mx, p_words0, p_words1, p_scales, c, p_bf[c][:])
+            if c > 0:
+                scores(c - 1)
+        scores(CHUNKS - 1)
+
+        numer = sb("numer", [P, CHUNKS, S], F32, tag="late")
+        for c in range(CHUNKS):
+            total = sb(f"total{c}", [P, 1], F32)
+            inverse = sb(f"inverse{c}", [P, 1], F32)
+            probs = sb(f"probs{c}", [P, S], F32)
+            nc.scalar.activation(out=numer[:, c, :], in_=logits[c][:], func=ACT.Exp, bias=neg_max[c][:], accum_out=total[:])
+            nc.vector.reciprocal(out=inverse[:], in_=total[:])
+            engine = nc.vector if c >= 3 else nc.gpsimd
+            engine.tensor_scalar(out=probs[:], in0=numer[:, c, :], scalar1=inverse[:], scalar2=0.0, op0=ALU.mult, op1=ALU.add)
+            nc.sync.dma_start(out=out[c * CHUNK : (c + 1) * CHUNK, :], in_=probs[:])

@@ -24,6 +24,7 @@ CHUNK = 128
 CHUNKS = S // CHUNK
 HALF = S // 2
 SLOT = 4 * T
+UNITS = H // 16
 
 
 def tile_picked_zarc_gelu_p_kernel(tc, x_words, x_scales, w1, w2, head, offs, dst, out):
@@ -51,21 +52,25 @@ def tile_picked_zarc_gelu_p_kernel(tc, x_words, x_scales, w1, w2, head, offs, ds
                 out=scale_table[32 * q : 32 * q + 4 * PASSES, :].bitcast(I32),
                 in_=x_scales[:, 4 * q : 4 * q + 4, :].bitcast(I32),
             )
-        head_table = sb("head_table", [P, T], F32)
-        nc.vector.memset(head_table[:], 0.0)
-        nc.sync.dma_start(out=head_table[0:1, :], in_=head[0:1, :])
         ident = sb("ident", [P, P], F32)
-        zeros = stage.tile([P, 3 * T], F32, name="zeros", offset=SLOT)
-        nc.vector.memset(zeros[:, 0:P], 0.0)
-        nc.gpsimd.affine_select(
-            out=ident[:],
-            in_=zeros[:, 0:P],
-            compare_op=ALU.not_equal,
-            fill=1.0,
-            base=0,
-            pattern=[[-1, P]],
-            channel_multiplier=1,
-        )
+
+        def identity_half(h, zeros):
+            nc.vector.memset(zeros[:, 0 : P // 2], 0.0)
+            nc.gpsimd.affine_select(
+                out=ident[:, h * P // 2 : (h + 1) * P // 2],
+                in_=zeros[:, 0 : P // 2],
+                compare_op=ALU.not_equal,
+                fill=1.0,
+                base=-h * P // 2,
+                pattern=[[-1, P // 2]],
+                channel_multiplier=1,
+            )
+
+        identity_half(0, stage.tile([P, T], F32, name="zeros0", offset=SLOT))
+        head_table = stage.tile([P, T], F32, name="head_table", offset=4 * SLOT)
+        nc.vector.memset(head_table[:].bitcast(I32), 0)
+        nc.sync.dma_start(out=head_table[0:1, :], in_=head[0:1, :])
+        identity_half(1, stage.tile([P, 2 * T], F32, name="zeros1", offset=2 * SLOT))
 
         def load_words(o, offset):
             table = stage.tile([P, T], U32, name=f"word_table{o}", offset=offset)
@@ -75,25 +80,20 @@ def tile_picked_zarc_gelu_p_kernel(tc, x_words, x_scales, w1, w2, head, offs, ds
             )
             return table
 
-        def load_weight(name, offset, w, o, c0, c1):
-            raw = stage.tile([P, PACK, c1 - c0], F32, name=name, offset=offset)
-            rows = w[o * K_PASS : (o + 1) * K_PASS, c0:c1]
+        def load_weight(name, offset, w, o):
+            raw = stage.tile([P, PACK, H], F32, name=name, offset=offset)
+            rows = w[o * K_PASS : (o + 1) * K_PASS, :]
             nc.sync.dma_start(out=raw[:], in_=rows.rearrange("(p j) c -> p j c", j=PACK))
             return raw
 
-        def load_halves(name, offset, w):
-            return [load_weight(f"{name}{h}", offset + h * SLOT // 2, w, 1, h * H // 2, (h + 1) * H // 2) for h in range(2)]
-
-        def round_weight(name, raw, vector_units):
-            width = raw.shape[2]
-            units = width // 16
-            rounded = sb(name, [P, PACK * width], BF16)
-            src = raw[:].rearrange("p j (u t i) -> p u t j i", t=4, i=4)
-            dst_view = rounded[:].rearrange("p (t u i j) -> p u t j i", t=4, i=4, j=4)
+        def round_weight(name, offset, raw, t0, t1, vector_units):
+            rounded = stage.tile([P, (t1 - t0) * K_PASS], BF16, name=name, offset=5 * SLOT + offset, align_bytes=64)
+            before = raw[:].rearrange("p j (u t i) -> p u t j i", t=4, i=4)[:, :, t0:t1]
+            after = rounded[:].rearrange("p (t u i j) -> p u t j i", u=UNITS, i=4, j=4)
             if vector_units > 0:
-                nc.vector.tensor_copy(out=dst_view[:, 0:vector_units], in_=src[:, 0:vector_units])
-            if vector_units < units:
-                nc.scalar.copy(out=dst_view[:, vector_units:units], in_=src[:, vector_units:units])
+                nc.vector.tensor_copy(out=after[:, 0:vector_units], in_=before[:, 0:vector_units])
+            if vector_units < UNITS:
+                nc.scalar.copy(out=after[:, vector_units:UNITS], in_=before[:, vector_units:UNITS])
             return rounded
 
         def mx_tiles(name, width):
@@ -102,37 +102,50 @@ def tile_picked_zarc_gelu_p_kernel(tc, x_words, x_scales, w1, w2, head, offs, ds
         def quantize(mx, c0, c1, values):
             nc.vector.quantize_mx(out=mx[0][:, c0:c1].bitcast(FP8X4), scales=mx[1][:, c0:c1], in_=values)
 
-        def quantize_half(mx, h, rounded):
-            for t in range(PACK):
-                c0 = t * P + h * P // 2
-                quantize(mx, c0, c0 + P // 2, rounded[:, t * 256 : (t + 1) * 256])
-
-        def gather(name, table, dtype, lst):
-            picked = sb(name, [P, 16 * lst.shape[1]], dtype)
+        def gather(picked, table, lst):
             nc.vector.tensor_copy(out=picked[:], in_=table[:].indirect(lst))
             return picked
 
-        def gather_half(name, table, lst, h):
-            return gather(f"{name}{h}", table, U32, lst[:, 16 * h : 16 * (h + 1)])
+        def half(lst, h):
+            return lst[:, 16 * h : 16 * (h + 1)]
 
         w2_mx = [mx_tiles(f"w2_mx{o}", H) for o in range(PASSES)]
         w1_mx = [mx_tiles(f"w1_mx{o}", H) for o in range(PASSES)]
 
-        w1_raw0 = load_weight("w1_raw0", 0, w1, 0, 0, H)
+        w1_raw0 = load_weight("w1_raw0", 0, w1, 0)
         words0 = load_words(0, SLOT)
-        w2_raw0 = load_weight("w2_raw0", 2 * SLOT, w2, 0, 0, H)
-        words1 = load_words(1, 3 * SLOT)
+        w2_raw0 = load_weight("w2_raw0", 2 * SLOT, w2, 0)
+        w2_raw1 = load_weight("w2_raw1", 3 * SLOT, w2, 1)
 
-        w1_bf0 = round_weight("w1_bf0", w1_raw0, 0)
-        w2_raw1 = load_halves("w2_raw1", 0, w2)
-        d_scales = gather("d_scales", scale_table, U8, dst_sb[:])
-        p_scales = gather("p_scales", scale_table, U8, offs_sb[:])
-        head_row = gather("head_row", head_table, F32, dst_sb[:])
+        w1_bf0 = round_weight("w1_bf0", 0, w1_raw0, 0, PACK, 0)
+        words1 = load_words(1, 0)
+        d_scales = gather(sb("d_scales", [P, S], U8), scale_table, dst_sb[:])
+        p_scales = gather(sb("p_scales", [P, S], U8), scale_table, offs_sb[:])
+        head_row = gather(sb("head_row", [P, S], F32), head_table, dst_sb[:])
+        w1_raw1 = load_weight("w1_raw1", 4 * SLOT, w1, 1)
 
         turned = bank("turned", "p0")
         for c in range(CHUNKS):
             nc.tensor.transpose(turned[:, c * P : (c + 1) * P], head_row[:, c * P : (c + 1) * P], ident[:])
-        head_col = sb("head_col", [P, CHUNKS], F32)
+        quantize(w1_mx[0], 0, H, w1_bf0[:])
+        d_words0 = gather(sb("d_words0", [P, S], U32), words0, dst_sb[:])
+        p_words0 = gather(sb("p_words0", [P, S], U32), words0, offs_sb[:])
+        w2_bf0 = round_weight("w2_bf0", 4096, w2_raw0, 0, PACK, 0)
+        quantize(w2_mx[0], 0, H, w2_bf0[:])
+        w2_bf1 = round_weight("w2_bf1", 8192, w2_raw1, 0, PACK, 12)
+        quantize(w2_mx[1], 0, H, w2_bf1[:])
+        for i in range(4):
+            warm = bank(f"warm{i}", f"p{2 + i % 2}")
+            nc.tensor.matmul_mx(
+                out=warm[:],
+                lhsT=w2_mx[0][0][:, 0:P].bitcast(FP8X4),
+                lhsT_scale=w2_mx[0][1][:, 0:P],
+                rhs=d_words0[:].bitcast(FP8X4),
+                rhs_scale=d_scales[:],
+                start=True,
+                stop=True,
+            )
+        head_col = stage.tile([P, CHUNKS], F32, name="head_col", offset=3 * SLOT)
         nc.scalar.copy(out=head_col[:], in_=turned[:, 0:S:P])
         spread = bank("spread", "p1")
         for c in range(CHUNKS):
@@ -140,27 +153,8 @@ def tile_picked_zarc_gelu_p_kernel(tc, x_words, x_scales, w1, w2, head, offs, ds
         head_all = sb("head_all", [P, S], F32)
         nc.scalar.copy(out=head_all[:], in_=spread[:])
 
-        d_words0 = gather("d_words0", words0, U32, dst_sb[:])
-        p_words0 = gather("p_words0", words0, U32, offs_sb[:])
-        quantize(w1_mx[0], 0, H, w1_bf0[:])
-        w2_bf0 = round_weight("w2_bf0", w2_raw0, 6)
-        w1_raw1 = load_halves("w1_raw1", 2 * SLOT, w1)
-        quantize(w2_mx[0], 0, H, w2_bf0[:])
-        d_words1 = [gather_half("d_words1", words1, dst_sb, h) for h in range(2)]
-        p_words1 = [gather_half("p_words1", words1, offs_sb, 0)]
-        for i in range(8):
-            warm = bank(f"warm{i}", f"p{2 + i % 2}")
-            nc.tensor.matmul_mx(
-                out=warm[:, 0:HALF],
-                lhsT=w2_mx[0][0][:, 0:P].bitcast(FP8X4),
-                lhsT_scale=w2_mx[0][1][:, 0:P],
-                rhs=d_words1[1][:].bitcast(FP8X4),
-                rhs_scale=d_scales[4:P, 1 * HALF : (1 + 1) * HALF],
-                start=True,
-                stop=True,
-            )
-        for h, vector_units in enumerate((0, 8)):
-            quantize_half(w2_mx[1], h, round_weight(f"w2_bf1{h}", w2_raw1[h], vector_units))
+        d_words1 = [gather(sb(f"d_words1{h}", [P, HALF], U32), words1, half(dst_sb, h)) for h in range(2)]
+        p_words1 = [gather(sb("p_words10", [P, HALF], U32), words1, half(offs_sb, 0))]
 
         def tower_chunk(acc, w_mx, picked0, picked1, picked_scales, c, hidden):
             cols = slice(c * CHUNK, (c + 1) * CHUNK)
@@ -187,15 +181,18 @@ def tile_picked_zarc_gelu_p_kernel(tc, x_words, x_scales, w1, w2, head, offs, ds
             part = d_bf[c // 2][:, (c % 2) * K_PASS : (c % 2 + 1) * K_PASS]
             tower_chunk(bank(f"d_acc{c}", f"d{c}"), w2_mx, d_words0, d_words1, d_scales, c, part)
 
-        for h, vector_units in enumerate((16, 16)):
-            quantize_half(w1_mx[1], h, round_weight(f"w1_bf1{h}", w1_raw1[h], vector_units))
-        p_words1.append(gather_half("p_words1", words1, offs_sb, 1))
+        w1_bf1 = [round_weight(f"w1_bf1{h}", 2048 * h, w1_raw1, 2 * h, 2 * h + 2, (UNITS, 24)[h]) for h in range(2)]
+        for h in range(2):
+            quantize(w1_mx[1], h * H // 2, (h + 1) * H // 2, w1_bf1[h][:])
 
-        d_mx = mx_tiles("d_mx", S)
+        late_words = stage.tile([P, HALF], U32, name="p_words11", offset=5 * SLOT + 2048, align_bytes=64)
+        p_words1.append(gather(late_words, words1, half(offs_sb, 1)))
+        d_codes = stage.tile([P, S], U32, name="d_codes", offset=5 * SLOT + 3072, align_bytes=64)
+        d_mx = (d_codes, sb("d_mx_scales", [P, S], U8))
         for h in range(2):
             quantize(d_mx, h * HALF, (h + 1) * HALF, d_bf[h][:])
 
-        p_bf = [sb(f"p_bf{c}", [P, K_PASS], BF16, tag="late" if c == CHUNKS - 1 else None) for c in range(CHUNKS)]
+        p_bf = [sb(f"p_bf{c}", [P, K_PASS], BF16) for c in range(CHUNKS)]
         p_mx = [mx_tiles(f"p_mx{c}", CHUNK) for c in range(CHUNKS)]
         logits = [sb(f"logits{c}", [P, S], F32) for c in range(CHUNKS)]
         neg_max = [sb(f"neg_max{c}", [P, 1], F32) for c in range(CHUNKS)]
@@ -212,22 +209,43 @@ def tile_picked_zarc_gelu_p_kernel(tc, x_words, x_scales, w1, w2, head, offs, ds
                 start=True,
                 stop=True,
             )
+            return acc
+
+        def logits_and_max(c, acc):
             nc.vector.tensor_tensor(out=logits[c][:], in0=acc[:], in1=head_all[:], op=ALU.add)
             nc.vector.tensor_reduce(out=neg_max[c][:], in_=logits[c][:], axis=AXIS.X, op=ALU.max, negate=True)
 
-        for c in range(CHUNKS):
+        def p_chunk(c):
             tower_chunk(bank(f"p_acc{c}", f"p{c}"), w1_mx, p_words0, p_words1, p_scales, c, p_bf[c][:])
-            if c > 0:
-                scores(c - 1)
-        scores(CHUNKS - 1)
 
-        numer = sb("numer", [P, CHUNKS, S], F32, tag="late")
-        for c in range(CHUNKS):
+        def exponentials(c, numer):
             total = sb(f"total{c}", [P, 1], F32)
             inverse = sb(f"inverse{c}", [P, 1], F32)
-            probs = sb(f"probs{c}", [P, S], F32)
             nc.scalar.activation(out=numer[:, c, :], in_=logits[c][:], func=ACT.Exp, bias=neg_max[c][:], accum_out=total[:])
             nc.vector.reciprocal(out=inverse[:], in_=total[:])
-            engine = nc.vector if c >= 3 else nc.gpsimd
+            return inverse
+
+        def normalise(c, engine, numer, inverse):
+            probs = sb(f"probs{c}", [P, S], F32)
             engine.tensor_scalar(out=probs[:], in0=numer[:, c, :], scalar1=inverse[:], scalar2=0.0, op0=ALU.mult, op1=ALU.add)
             nc.sync.dma_start(out=out[c * CHUNK : (c + 1) * CHUNK, :], in_=probs[:])
+
+        p_chunk(0)
+        p_chunk(1)
+        p_chunk(2)
+        y_acc = [scores(0)]
+        p_chunk(3)
+        table_switch = sb("table_switch", [P, 1], F32, tag="late")
+        nc.scalar.activation(out=table_switch[:], in_=p_bf[CHUNKS - 1][:, 0:1], func=ACT.Exp, scale=0.0)
+        y_acc.append(scores(1))
+        logits_and_max(0, y_acc[0])
+        y_acc.append(scores(2))
+        y_acc.append(scores(3))
+        numer = sb("numer", [P, CHUNKS, S], F32, tag="late")
+        logits_and_max(1, y_acc[1])
+        for c in range(2):
+            inverse = exponentials(c, numer)
+            normalise(c, nc.gpsimd, numer, inverse)
+            logits_and_max(c + 2, y_acc[c + 2])
+        for c in range(2, CHUNKS):
+            normalise(c, nc.vector, numer, exponentials(c, numer))

@@ -128,6 +128,12 @@ def tile_picked_zarc_gelu_p_kernel(tc, x_words, x_scales, w1, w2, head, offs, ds
         for c in range(CHUNKS):
             nc.tensor.transpose(turned[:, c * P : (c + 1) * P], head_row[:, c * P : (c + 1) * P], ident[:])
         quantize(w1_mx[0], 0, H, w1_bf0[:])
+        head_col = sb("head_col", [P, CHUNKS], F32)
+        nc.vector.tensor_copy(out=head_col[:], in_=turned[:, 0:S:P])
+        spread = bank("spread", "p3")
+        for c in range(CHUNKS):
+            nc.tensor.transpose(spread[:, c * P : (c + 1) * P], head_col[:, c : c + 1].to_broadcast([P, P]), ident[:])
+
         d_words0 = gather(sb("d_words0", [P, S], U32), words0, dst_sb[:])
         p_words0 = gather(sb("p_words0", [P, S], U32), words0, offs_sb[:])
         w2_bf0 = round_weight("w2_bf0", 4096, w2_raw0, 0, PACK, 0)
@@ -135,7 +141,7 @@ def tile_picked_zarc_gelu_p_kernel(tc, x_words, x_scales, w1, w2, head, offs, ds
         w2_bf1 = round_weight("w2_bf1", 8192, w2_raw1, 0, PACK, 12)
         quantize(w2_mx[1], 0, H, w2_bf1[:])
         for i in range(4):
-            warm = bank(f"warm{i}", f"p{2 + i % 2}")
+            warm = bank(f"warm{i}", f"p{1 + i % 2}")
             nc.tensor.matmul_mx(
                 out=warm[:],
                 lhsT=w2_mx[0][0][:, 0:P].bitcast(FP8X4),
@@ -145,14 +151,8 @@ def tile_picked_zarc_gelu_p_kernel(tc, x_words, x_scales, w1, w2, head, offs, ds
                 start=True,
                 stop=True,
             )
-        head_col = stage.tile([P, CHUNKS], F32, name="head_col", offset=3 * SLOT)
-        nc.scalar.copy(out=head_col[:], in_=turned[:, 0:S:P])
-        spread = bank("spread", "p1")
-        for c in range(CHUNKS):
-            nc.tensor.transpose(spread[:, c * P : (c + 1) * P], head_col[:, c : c + 1].to_broadcast([P, P]), ident[:])
-        head_all = sb("head_all", [P, S], F32)
+        head_all = stage.tile([P, S], F32, name="head_all", offset=3 * SLOT)
         nc.scalar.copy(out=head_all[:], in_=spread[:])
-
         d_words1 = [gather(sb(f"d_words1{h}", [P, HALF], U32), words1, half(dst_sb, h)) for h in range(2)]
         p_words1 = [gather(sb("p_words10", [P, HALF], U32), words1, half(offs_sb, 0))]
 
@@ -181,7 +181,7 @@ def tile_picked_zarc_gelu_p_kernel(tc, x_words, x_scales, w1, w2, head, offs, ds
             part = d_bf[c // 2][:, (c % 2) * K_PASS : (c % 2 + 1) * K_PASS]
             tower_chunk(bank(f"d_acc{c}", f"d{c}"), w2_mx, d_words0, d_words1, d_scales, c, part)
 
-        w1_bf1 = [round_weight(f"w1_bf1{h}", 2048 * h, w1_raw1, 2 * h, 2 * h + 2, (UNITS, 24)[h]) for h in range(2)]
+        w1_bf1 = [round_weight(f"w1_bf1{h}", 2048 * h, w1_raw1, 2 * h, 2 * h + 2, (UNITS, 32)[h]) for h in range(2)]
         for h in range(2):
             quantize(w1_mx[1], h * H // 2, (h + 1) * H // 2, w1_bf1[h][:])
 
@@ -225,9 +225,12 @@ def tile_picked_zarc_gelu_p_kernel(tc, x_words, x_scales, w1, w2, head, offs, ds
             nc.vector.reciprocal(out=inverse[:], in_=total[:])
             return inverse
 
-        def normalise(c, engine, numer, inverse):
+        def normalise(c, numer, inverse):
             probs = sb(f"probs{c}", [P, S], F32)
-            engine.tensor_scalar(out=probs[:], in0=numer[:, c, :], scalar1=inverse[:], scalar2=0.0, op0=ALU.mult, op1=ALU.add)
+            if c < 1:
+                nc.scalar.activation(out=probs[:], in_=numer[:, c, :], func=ACT.Copy, scale=inverse[:])
+            else:
+                nc.vector.tensor_scalar(out=probs[:], in0=numer[:, c, :], scalar1=inverse[:], scalar2=None, op0=ALU.mult)
             nc.sync.dma_start(out=out[c * CHUNK : (c + 1) * CHUNK, :], in_=probs[:])
 
         p_chunk(0)
@@ -243,9 +246,12 @@ def tile_picked_zarc_gelu_p_kernel(tc, x_words, x_scales, w1, w2, head, offs, ds
         y_acc.append(scores(3))
         numer = sb("numer", [P, CHUNKS, S], F32, tag="late")
         logits_and_max(1, y_acc[1])
-        for c in range(2):
-            inverse = exponentials(c, numer)
-            normalise(c, nc.gpsimd, numer, inverse)
-            logits_and_max(c + 2, y_acc[c + 2])
+        inverse = exponentials(0, numer)
+        logits_and_max(2, y_acc[2])
+        inverses = [exponentials(1, numer)]
+        normalise(0, numer, inverse)
+        logits_and_max(3, y_acc[3])
         for c in range(2, CHUNKS):
-            normalise(c, nc.vector, numer, exponentials(c, numer))
+            inverses.append(exponentials(c, numer))
+        for c in range(1, CHUNKS):
+            normalise(c, numer, inverses[c - 1])

from contextlib import ExitStack

import concourse.mybir as mybir

K, T, S, H = 1024, 2048, 512, 512
FLOPS = 2 * (2 * K * H * S) + 2 * H * S * S

F32 = mybir.dt.float32
BF16 = mybir.dt.bfloat16
I32 = mybir.dt.int32
U32 = mybir.dt.uint32
U16 = mybir.dt.uint16
U8 = mybir.dt.uint8
FP8X4 = mybir.dt.float8_e4m3fn_x4
ACT = mybir.ActivationFunctionType
ALU = mybir.AluOpType
AXIS = mybir.AxisListType

P = 128
PACK = 4
K_PASS = P * PACK
PASSES = K // K_PASS
CHUNK = 128
CHUNKS = S // CHUNK
HALF = S // 2
SLOT = 4 * T
UNITS = H // 16


def tile_picked_zarc_gelu_p_kernel(tc, x_words, x_scales, w1, w2, head, offs, dst, out):
    nc = tc.nc
    with ExitStack() as ctx:
        keep = ctx.enter_context(tc.tile_pool(name="keep", bufs=1))
        stage = ctx.enter_context(tc.tile_pool(name="stage", bufs=1))
        psum = ctx.enter_context(tc.psum_pool(name="psum", bufs=1))

        def sb(name, shape, dtype, tag=None):
            return keep.tile(shape, dtype, name=name, tag=tag or name, align_bytes=64)

        def bank(name, tag):
            return psum.tile([P, S], F32, name=name, tag=tag)

        offs_sb = keep.tile([P, S // 16], U16, name="offs_sb")
        dst_sb = keep.tile([P, S // 16], U16, name="dst_sb")
        nc.sync.dma_start(offs_sb[:], offs)
        nc.sync.dma_start(dst_sb[:], dst)

        scale_table = sb("scale_table", [P, T], U8)
        nc.vector.memset(scale_table[:].bitcast(I32), 0)
        for q in range(4):
            nc.scalar.dma_start(
                out=scale_table[32 * q : 32 * q + 4 * PASSES, :].bitcast(I32),
                in_=x_scales[:, 4 * q : 4 * q + 4, :].bitcast(I32),
            )
        ident = sb("ident", [P, P], F32)

        def identity_half(h, zeros):
            nc.vector.memset(zeros[:, 0 : P // 2], 0.0)
            nc.gpsimd.affine_select(
                out=ident[:, h * P // 2 : (h + 1) * P // 2],
                in_=zeros[:, 0 : P // 2],
                compare_op=ALU.not_equal,
                fill=1.0,
                base=-h * P // 2,
                pattern=[[-1, P // 2]],
                channel_multiplier=1,
            )

        identity_half(0, stage.tile([P, T], F32, name="zeros0", offset=SLOT))
        head_table = stage.tile([P, T], F32, name="head_table", offset=4 * SLOT)
        nc.vector.memset(head_table[:].bitcast(I32), 0)
        nc.sync.dma_start(out=head_table[0:1, :], in_=head[0:1, :])
        identity_half(1, stage.tile([P, 2 * T], F32, name="zeros1", offset=2 * SLOT))

        def load_words(o, offset):
            table = stage.tile([P, T], U32, name=f"word_table{o}", offset=offset)
            nc.sync.dma_start(
                out=table[:].bitcast(I32),
                in_=x_words[o].rearrange("p n r -> p (n r)").bitcast(I32),
            )
            return table

        def load_weight(name, offset, w, o):
            raw = stage.tile([P, PACK, H], F32, name=name, offset=offset)
            rows = w[o * K_PASS : (o + 1) * K_PASS, :]
            nc.sync.dma_start(out=raw[:], in_=rows.rearrange("(p j) c -> p j c", j=PACK))
            return raw

        def round_weight(name, offset, raw, t0, t1, vector_units):
            rounded = stage.tile([P, (t1 - t0) * K_PASS], BF16, name=name, offset=5 * SLOT + offset, align_bytes=64)
            before = raw[:].rearrange("p j (u t i) -> p u t j i", t=4, i=4)[:, :, t0:t1]
            after = rounded[:].rearrange("p (t u i j) -> p u t j i", u=UNITS, i=4, j=4)
            if vector_units > 0:
                nc.vector.tensor_copy(out=after[:, 0:vector_units], in_=before[:, 0:vector_units])
            if vector_units < UNITS:
                nc.scalar.copy(out=after[:, vector_units:UNITS], in_=before[:, vector_units:UNITS])
            return rounded

        def mx_tiles(name, width):
            return sb(name + "_codes", [P, width], U32), sb(name + "_scales", [P, width], U8)

        def quantize(mx, c0, c1, values):
            nc.vector.quantize_mx(out=mx[0][:, c0:c1].bitcast(FP8X4), scales=mx[1][:, c0:c1], in_=values)

        def gather(picked, table, lst):
            nc.vector.tensor_copy(out=picked[:], in_=table[:].indirect(lst))
            return picked

        def half(lst, h):
            return lst[:, 16 * h : 16 * (h + 1)]

        w2_mx = [mx_tiles(f"w2_mx{o}", H) for o in range(PASSES)]
        w1_mx = [mx_tiles(f"w1_mx{o}", H) for o in range(PASSES)]

        w1_raw0 = load_weight("w1_raw0", 0, w1, 0)
        words0 = load_words(0, SLOT)
        w2_raw0 = load_weight("w2_raw0", 2 * SLOT, w2, 0)
        w2_raw1 = load_weight("w2_raw1", 3 * SLOT, w2, 1)

        w1_bf0 = round_weight("w1_bf0", 0, w1_raw0, 0, PACK, 0)
        words1 = load_words(1, 0)
        d_scales = gather(sb("d_scales", [P, S], U8), scale_table, dst_sb[:])
        p_scales = gather(sb("p_scales", [P, S], U8), scale_table, offs_sb[:])
        head_row = gather(sb("head_row", [P, S], F32), head_table, dst_sb[:])
        w1_raw1 = load_weight("w1_raw1", 4 * SLOT, w1, 1)

        turned = bank("turned", "p0")
        for c in range(CHUNKS):
            nc.tensor.transpose(turned[:, c * P : (c + 1) * P], head_row[:, c * P : (c + 1) * P], ident[:])
        quantize(w1_mx[0], 0, H, w1_bf0[:])
        head_col = sb("head_col", [P, CHUNKS], F32)
        nc.vector.tensor_copy(out=head_col[:], in_=turned[:, 0:S:P])
        spread = bank("spread", "p3")
        for c in range(CHUNKS):
            nc.tensor.transpose(spread[:, c * P : (c + 1) * P], head_col[:, c : c + 1].to_broadcast([P, P]), ident[:])

        d_words0 = gather(sb("d_words0", [P, S], U32), words0, dst_sb[:])
        p_words0 = gather(sb("p_words0", [P, S], U32), words0, offs_sb[:])
        w2_bf0 = round_weight("w2_bf0", 4096, w2_raw0, 0, PACK, 0)
        quantize(w2_mx[0], 0, H, w2_bf0[:])
        w2_bf1 = round_weight("w2_bf1", 8192, w2_raw1, 0, PACK, 12)
        quantize(w2_mx[1], 0, H, w2_bf1[:])
        for i in range(4):
            warm = bank(f"warm{i}", f"p{1 + i % 2}")
            nc.tensor.matmul_mx(
                out=warm[:],
                lhsT=w2_mx[0][0][:, 0:P].bitcast(FP8X4),
                lhsT_scale=w2_mx[0][1][:, 0:P],
                rhs=d_words0[:].bitcast(FP8X4),
                rhs_scale=d_scales[:],
                start=True,
                stop=True,
            )
        head_all = stage.tile([P, S], F32, name="head_all", offset=3 * SLOT)
        nc.scalar.copy(out=head_all[:], in_=spread[:])
        d_words1 = [gather(sb(f"d_words1{h}", [P, HALF], U32), words1, half(dst_sb, h)) for h in range(2)]
        p_words1 = [gather(sb("p_words10", [P, HALF], U32), words1, half(offs_sb, 0))]

        def tower_chunk(acc, w_mx, picked0, picked1, picked_scales, c, hidden):
            cols = slice(c * CHUNK, (c + 1) * CHUNK)
            moving = (picked0[:, cols], picked1[c // 2][:, (c % 2) * CHUNK : (c % 2 + 1) * CHUNK])
            for t in range(PACK):
                for o in range(PASSES):
                    nc.tensor.matmul_mx(
                        out=acc[:, t * CHUNK : (t + 1) * CHUNK],
                        lhsT=w_mx[o][0][:, t * P : (t + 1) * P].bitcast(FP8X4),
                        lhsT_scale=w_mx[o][1][:, t * P : (t + 1) * P],
                        rhs=moving[o].bitcast(FP8X4),
                        rhs_scale=picked_scales[4 * o : P, cols],
                        start=(o == 0),
                        stop=(o == PASSES - 1),
                    )
            nc.scalar.activation(
                out=hidden.rearrange("p (n t) -> p n t", t=PACK),
                in_=acc[:].rearrange("p (t n) -> p n t", t=PACK),
                func=ACT.Gelu_apprx_tanh,
            )

        d_bf = [sb(f"d_bf{h}", [P, PACK * HALF], BF16) for h in range(2)]
        for c in range(CHUNKS):
            part = d_bf[c // 2][:, (c % 2) * K_PASS : (c % 2 + 1) * K_PASS]
            tower_chunk(bank(f"d_acc{c}", f"d{c}"), w2_mx, d_words0, d_words1, d_scales, c, part)

        w1_bf1 = [round_weight(f"w1_bf1{h}", 2048 * h, w1_raw1, 2 * h, 2 * h + 2, (UNITS, 32)[h]) for h in range(2)]
        for h in range(2):
            quantize(w1_mx[1], h * H // 2, (h + 1) * H // 2, w1_bf1[h][:])

        late_words = stage.tile([P, HALF], U32, name="p_words11", offset=5 * SLOT + 2048, align_bytes=64)
        p_words1.append(gather(late_words, words1, half(offs_sb, 1)))
        d_codes = stage.tile([P, S], U32, name="d_codes", offset=5 * SLOT + 3072, align_bytes=64)
        d_mx = (d_codes, sb("d_mx_scales", [P, S], U8))
        for h in range(2):
            quantize(d_mx, h * HALF, (h + 1) * HALF, d_bf[h][:])

        p_bf = [sb(f"p_bf{c}", [P, K_PASS], BF16) for c in range(CHUNKS)]
        p_mx = [mx_tiles(f"p_mx{c}", CHUNK) for c in range(CHUNKS)]
        logits = [sb(f"logits{c}", [P, S], F32) for c in range(CHUNKS)]
        neg_max = [sb(f"neg_max{c}", [P, 1], F32) for c in range(CHUNKS)]

        def scores(c):
            quantize(p_mx[c], 0, CHUNK, p_bf[c][:])
            acc = bank(f"y_acc{c}", f"d{c}")
            nc.tensor.matmul_mx(
                out=acc[:],
                lhsT=p_mx[c][0][:].bitcast(FP8X4),
                lhsT_scale=p_mx[c][1][:],
                rhs=d_mx[0][:].bitcast(FP8X4),
                rhs_scale=d_mx[1][:],
                start=True,
                stop=True,
            )
            return acc

        def logits_and_max(c, acc):
            nc.vector.tensor_tensor(out=logits[c][:], in0=acc[:], in1=head_all[:], op=ALU.add)
            nc.vector.tensor_reduce(out=neg_max[c][:], in_=logits[c][:], axis=AXIS.X, op=ALU.max, negate=True)

        def p_chunk(c):
            tower_chunk(bank(f"p_acc{c}", f"p{c}"), w1_mx, p_words0, p_words1, p_scales, c, p_bf[c][:])

        def exponentials(c, numer):
            total = sb(f"total{c}", [P, 1], F32)
            inverse = sb(f"inverse{c}", [P, 1], F32)
            nc.scalar.activation(out=numer[:, c, :], in_=logits[c][:], func=ACT.Exp, bias=neg_max[c][:], accum_out=total[:])
            nc.vector.reciprocal(out=inverse[:], in_=total[:])
            return inverse

        def normalise(c, numer, inverse):
            probs = sb(f"probs{c}", [P, S], F32)
            if c < 1:
                nc.scalar.activation(out=probs[:], in_=numer[:, c, :], func=ACT.Copy, scale=inverse[:])
            else:
                nc.vector.tensor_scalar(out=probs[:], in0=numer[:, c, :], scalar1=inverse[:], scalar2=None, op0=ALU.mult)
            nc.sync.dma_start(out=out[c * CHUNK : (c + 1) * CHUNK, :], in_=probs[:])

        p_chunk(0)
        p_chunk(1)
        p_chunk(2)
        y_acc = [scores(0)]
        p_chunk(3)
        table_switch = sb("table_switch", [P, 1], F32, tag="late")
        nc.scalar.activation(out=table_switch[:], in_=p_bf[CHUNKS - 1][:, 0:1], func=ACT.Exp, scale=0.0)
        y_acc.append(scores(1))
        logits_and_max(0, y_acc[0])
        y_acc.append(scores(2))
        y_acc.append(scores(3))
        numer = sb("numer", [P, CHUNKS, S], F32, tag="late")
        logits_and_max(1, y_acc[1])
        inverse = exponentials(0, numer)
        logits_and_max(2, y_acc[2])
        inverses = [exponentials(1, numer)]
        normalise(0, numer, inverse)
        logits_and_max(3, y_acc[3])
        for c in range(2, CHUNKS):
            inverses.append(exponentials(c, numer))
        for c in range(1, CHUNKS):
            normalise(c, numer, inverses[c - 1])
